import numpy as np
import ml_dtypes


def mxq(x, axis, fmt="e4m3"):
    dtype, down = {"e4m3": (ml_dtypes.float8_e4m3fn, 7), "e5m2": (ml_dtypes.float8_e5m2, 14)}[fmt]
    v = np.moveaxis(np.asarray(x, np.float32).astype(ml_dtypes.bfloat16).astype(np.float64), axis, -1)
    blocks = v.reshape(v.shape[:-1] + (-1, 32))
    amax = np.abs(blocks).max(-1, keepdims=True)
    byte = np.maximum(np.where(amax > 0, np.frexp(amax)[1] - 1 + 127, 0) - down, 1)
    scale = np.exp2(byte - 127.0)
    codes = (blocks / scale).astype(np.float32).astype(dtype).astype(np.float64)
    return np.moveaxis((codes * scale).reshape(v.shape), -1, axis)


WIDE = False


def mx_kscale(k):
    if not WIDE:
        return np.ones(k)
    levels = np.array([10, -10, 5, -5, 0])
    if k % 512:
        return np.exp2(np.random.permutation(np.resize(levels, k // 32))).repeat(32)
    a = np.empty((k // 512, 16))
    for p in range(k // 512):
        a[p, :8] = np.random.permutation(np.resize(levels, 8))
        for g in range(8):
            far = levels[np.abs(levels - a[p, g]) >= 10]
            a[p, g + 8] = far[np.random.randint(len(far))]
    return np.exp2(a.ravel()).repeat(32)


BF16 = ml_dtypes.bfloat16


def bf(x):
    return np.asarray(x, np.float32).astype(BF16)


def f64(x):
    return np.asarray(x).astype(np.float64)

def planes(Y):
    n, m = Y.shape
    b = f64(bf(Y)).reshape(n // 32, 32, m)
    amax = np.abs(b).max(1)
    byte = np.clip(np.where(amax > 0, np.frexp(amax)[1] - 1 + 127 - 7, 1), 1, 254)
    codes = (b * np.exp2(127.0 - byte)[:, None, :]).reshape(n, m).astype(np.float32).astype(ml_dtypes.float8_e4m3fn).view(np.uint8)
    words = codes.reshape(n // 512, 128, 4, m).transpose(0, 1, 3, 2)
    return np.ascontiguousarray(words), np.ascontiguousarray(byte.astype(np.uint8).reshape(n // 512, 16, m))


P, T, F, D = 2, 2048, 1024, 1024


def setup_inputs():
    s = mx_kscale(T)
    omega = np.pi * (np.arange(F) + 0.25 + 0.5 * np.random.rand(F)) / F
    angle = omega[:, None] * (np.arange(T) + 0.5)[None, :]
    waves = np.sqrt(2.0 / T) * np.stack([np.cos(angle), np.sin(angle)])
    tokens = np.random.randn(T, D)
    strength = np.exp(0.8 * np.random.randn(F))
    filt = strength[:, None] * (1.0 + 0.3 * np.random.randn(F, D))
    offset = 0.4 * strength[None, :] * np.random.randn(P, F)
    return {
        "tokens": bf(tokens / s[:, None]),
        "waves": bf(waves * s[None, None, :]),
        "filt": bf(filt),
        "offset": bf(offset),
    }


def reference(tokens, waves, filt, offset):
    qw = mxq(f64(waves).reshape(P * F, T), 1, "e4m3")
    qx = mxq(f64(tokens), 0, "e4m3")
    z = (qw @ qx).reshape(P, F, D)
    y = z * f64(filt)[None, :, :] + f64(offset)[:, :, None]
    Y = y.transpose(1, 0, 2).reshape(F, P * D)
    words, scales = planes(Y)
    return y, words, scales

@@ -1,0 +1,301 @@
+from contextlib import ExitStack
+
+import concourse.mybir as mybir
+from concourse.masks import make_identity
+
+PARTS, T, F, D = 2, 2048, 1024, 1024
+FLOPS = 2 * PARTS * F * T * D
+
+F32 = mybir.dt.float32
+BF16 = mybir.dt.bfloat16
+I32 = mybir.dt.int32
+U8 = mybir.dt.uint8
+FP8X4 = mybir.dt.float8_e4m3fn_x4
+ALU = mybir.AluOpType
+IDENTITY = mybir.ActivationFunctionType.Identity
+
+P = 128
+PACK = 4
+K_PASS = P * PACK
+PASSES = T // K_PASS
+HALF = 512
+TILES = 16
+W_RING, X_RING, WG_RING, XG_RING, Y_RING, YG_RING = 8, 4, 3, 3, 4, 3
+
+
+def tile_nonuniform_fourier_filter_g2_kernel(tc, tokens, waves, filt, offset, out_0, out_1, out_2):
+    nc = tc.nc
+    with ExitStack() as ctx:
+        sb = ctx.enter_context(tc.tile_pool(name="sb", bufs=1))
+        ps = ctx.enter_context(tc.psum_pool(name="ps", bufs=1))
+        ctx.enter_context(tc.manual_schedule())
+
+        ident = sb.tile([P, P], F32, name="ident", align_bytes=64)
+        off_raw = sb.tile([P, 4, PACK], BF16, name="off_raw")
+        off = sb.tile([P, 4, PACK], F32, name="off")
+        w_codes = sb.tile([P, TILES, PASSES * P], I32, name="w_codes", align_bytes=64)
+        w_scales = sb.tile([P, TILES, PASSES * P], U8, name="w_scales", align_bytes=64)
+        x_codes = sb.tile([P, 2 * PASSES, HALF], I32, name="x_codes", align_bytes=64)
+        x_scales = sb.tile([P, 2 * PASSES, HALF], U8, name="x_scales", align_bytes=64)
+        filt_sb = sb.tile([P, 4, PACK, HALF], BF16, name="filt_sb", align_bytes=64)
+        y_words = sb.tile([P, 2, PARTS * D], I32, name="y_words", align_bytes=64)
+        y_scales = sb.tile([P, 2, PARTS * D], U8, name="y_scales", align_bytes=64)
+
+        w_raw, x_raw, w_bank, w_grouped, x_grouped, acc, y, y_grouped = {}, {}, {}, {}, {}, {}, {}, {}
+
+        def part_group(i):
+            return (i // 4) % 2, i // 8, i % 4
+
+        def load_w(i):
+            c, g, t = part_group(i)
+            w_raw[i] = sb.tile([P, T], BF16, name="w_raw%d" % (i % W_RING), align_bytes=64)
+            rows = waves[c, g * K_PASS:(g + 1) * K_PASS, :].rearrange("(m t) k -> m t k", t=PACK)
+            nc.sync.dma_start(out=w_raw[i][:], in_=rows[:, t, :])
+
+        def load_x(h, g):
+            x_raw[h, g] = sb.tile([P, PACK, HALF], BF16, name="x_raw%d" % (g % X_RING), align_bytes=64)
+            rows = tokens[g * K_PASS:(g + 1) * K_PASS, h * HALF:(h + 1) * HALF]
+            nc.sync.dma_start(out=x_raw[h, g][:], in_=rows.rearrange("(p j) w -> p j w", j=PACK))
+
+        def load_f(g, h, t0, t1):
+            rows = filt[g * K_PASS:(g + 1) * K_PASS, h * HALF:(h + 1) * HALF].rearrange("(p t) d -> p t d", t=PACK)
+            nc.sync.dma_start(out=filt_sb[:, 2 * g + h, t0:t1, :], in_=rows[:, t0:t1, :])
+
+        def transpose_w(i):
+            words = w_raw[i][:].bitcast(F32)
+            for b in range(2):
+                w_bank[i, b] = ps.tile([P, 2, 2, P], F32, name="bank%d" % (2 * (i % 2) + b))
+                for gg in range(2):
+                    g = 2 * b + gg
+                    for u in range(2):
+                        nc.tensor.transpose(w_bank[i, b][:, gg, u, :], words[:, 256 * g + u:256 * (g + 1):2], ident[:])
+
+        def evac_w(i):
+            w_grouped[i] = sb.tile([P, PASSES, P, 2], F32, name="w_grouped%d" % (i % WG_RING), align_bytes=64)
+            for b in range(2):
+                nc.scalar.copy(out=w_grouped[i][:, 2 * b:2 * b + 2, :, :], in_=w_bank[i, b][:].rearrange("p g u r -> p g r u"))
+
+        def quant_w(i):
+            nc.vector.quantize_mx(out=w_codes[:, i, :].bitcast(FP8X4), scales=w_scales[:, i, :],
+                                  in_=w_grouped[i][:].rearrange("p g r u -> p (g r u)").bitcast(BF16))
+
+        def weave(on_vector, dst, src, c0, c1):
+            o = dst[:, c0:c1, :].rearrange("p (c i) t -> p c t i", i=4)
+            s = src[:, :, c0:c1].rearrange("p t (c i) -> p c t i", i=4)
+            if on_vector:
+                nc.vector.tensor_copy(out=o, in_=s)
+            else:
+                nc.scalar.copy(out=o, in_=s)
+
+        def weave_x(h, g, split):
+            x_grouped[h, g] = sb.tile([P, HALF, PACK], BF16, name="x_grouped%d" % ((4 * h + g) % XG_RING), align_bytes=64)
+            weave(False, x_grouped[h, g], x_raw[h, g], 0, split)
+            weave(True, x_grouped[h, g], x_raw[h, g], split, HALF)
+
+        def quant_x(h, g):
+            nc.vector.quantize_mx(out=x_codes[:, 4 * h + g, :].bitcast(FP8X4), scales=x_scales[:, 4 * h + g, :],
+                                  in_=x_grouped[h, g][:].rearrange("p w j -> p (w j)"))
+
+        def mm(i, d0, width, g, bank):
+            h, c0 = divmod(d0, HALF)
+            if g == 0:
+                acc[i, d0] = ps.tile([P, width], F32, name="bank%d" % bank)
+            nc.tensor.matmul_mx(out=acc[i, d0][:],
+                                lhsT=w_codes[:, i, g * P:(g + 1) * P].bitcast(FP8X4),
+                                lhsT_scale=w_scales[:, i, g * P:(g + 1) * P],
+                                rhs=x_codes[:, 4 * h + g, c0:c0 + width].bitcast(FP8X4),
+                                rhs_scale=x_scales[:, 4 * h + g, c0:c0 + width],
+                                start=(g == 0), stop=(g == PASSES - 1))
+
+        def mm_all(i, d0, width, bank):
+            for g in range(PASSES):
+                mm(i, d0, width, g, bank)
+
+        def mul(i, d0, width):
+            c, g, t = part_group(i)
+            h, c0 = divmod(d0, HALF)
+            unit = (i // 4, h)
+            if unit not in y:
+                y[unit] = sb.tile([P, PACK, HALF], F32, name="y%d" % (len(y) % Y_RING), align_bytes=64)
+            nc.vector.tensor_tensor(out=y[unit][:, t, c0:c0 + width], in0=acc[i, d0][:],
+                                    in1=filt_sb[:, 2 * g + h, t, c0:c0 + width], op=ALU.mult)
+
+        def add(i, d0, width, on_vector):
+            c, g, t = part_group(i)
+            h, c0 = divmod(d0, HALF)
+            v = y[i // 4, h][:, t, c0:c0 + width]
+            col = off[:, 2 * c + g, t:t + 1]
+            if on_vector:
+                nc.vector.tensor_scalar(out=v, in0=v, scalar1=col, scalar2=None, op0=ALU.add)
+            else:
+                nc.scalar.activation(out=v, in_=v, func=IDENTITY, bias=col, scale=1.0)
+
+        def store_y(u, h, t0, t1, c0, c1):
+            c, g, t = part_group(4 * u)
+            rows = out_0[c, g * K_PASS:(g + 1) * K_PASS, h * HALF + c0:h * HALF + c1].rearrange("(p t) d -> p t d", t=PACK)
+            nc.sync.dma_start(out=rows[:, t0:t1, :], in_=y[u, h][:, t0:t1, c0:c1])
+
+        def weave_y(u, h, on_vector, c0, c1):
+            if (u, h) not in y_grouped:
+                y_grouped[u, h] = sb.tile([P, HALF, PACK], BF16, name="y_grouped%d" % (len(y_grouped) % YG_RING), align_bytes=64)
+            weave(on_vector, y_grouped[u, h], y[u, h], c0, c1)
+
+        def quant_y(u, h, c0, c1):
+            c, g, t = part_group(4 * u)
+            m0 = c * D + h * HALF
+            nc.vector.quantize_mx(out=y_words[:, g, m0 + c0:m0 + c1].bitcast(FP8X4), scales=y_scales[:, g, m0 + c0:m0 + c1],
+                                  in_=y_grouped[u, h][:, c0:c1, :].rearrange("p w j -> p (w j)"))
+
+        def store_words(u, h, c0, c1):
+            c, g, t = part_group(4 * u)
+            m0 = c * D + h * HALF
+            dst = out_1[g].rearrange("p m t -> p (m t)").bitcast(I32)
+            nc.sync.dma_start(out=dst[:, m0 + c0:m0 + c1], in_=y_words[:, g, m0 + c0:m0 + c1])
+
+        def store_scales(g, m0, m1, queues):
+            for q in range(4):
+                queues[q].dma_start(out=out_2[g, 4 * q:4 * q + 4, m0:m1].bitcast(I32),
+                                    in_=y_scales[32 * q:32 * q + 4, g, m0:m1].bitcast(I32))
+
+        make_identity(nc, ident[:])
+        nc.scalar.dma_start(out=off_raw[:], in_=offset.rearrange("c f -> (c f)").rearrange("(q p t) -> p q t", p=P, t=PACK))
+        for g in range(PASSES):
+            load_w(g)
+            load_x(0, g)
+        load_w(4)
+        load_w(5)
+        load_w(6)
+        load_f(0, 0, 0, 2)
+        load_w(7)
+        load_f(0, 0, 2, 4)
+        nc.scalar.activation(out=off[:], in_=off_raw[:], func=IDENTITY)
+
+        transpose_w(0)
+        for g in range(PASSES):
+            evac_w(g)
+            weave_x(0, g, 160)
+            quant_w(g)
+            quant_x(0, g)
+            transpose_w(g + 1)
+            if g == PASSES - 1:
+                transpose_w(5)
+            for gg in range(g):
+                mm(g, 0, HALF, gg, 4 + g)
+            for i in range(g + 1):
+                mm(i, 0, HALF, g, 4 + i)
+        evac_w(4)
+        evac_w(5)
+        quant_w(4)
+        quant_w(5)
+
+        load_w(8)
+        load_w(9)
+        load_x(1, 0)
+        for r in range(1, 6):
+            a, m = 2 * r + 4, 2 * r + 2
+            done = [0, 1, 2, 3] if r == 1 else [2 * r, 2 * r + 1]
+            transpose_w(a)
+            transpose_w(a + 1)
+            for i in done:
+                mul(i, 0, HALF)
+            mm_all(m, 0, HALF, 4 + m % 4)
+            mm_all(m + 1, 0, HALF, 4 + (m + 1) % 4)
+            evac_w(a)
+            evac_w(a + 1)
+            if r == 1:
+                add(0, 0, HALF, True)
+                add(1, 0, HALF, True)
+                quant_w(a)
+                add(2, 0, HALF, False)
+                add(3, 0, HALF, False)
+                quant_w(a + 1)
+                load_w(10)
+                load_w(11)
+                load_x(1, 1)
+                store_y(0, 0, 0, 4, 0, HALF)
+            else:
+                u, c0 = (r - 2) // 2, 256 * (r % 2)
+                weave_y(u, 0, True, c0, c0 + 256)
+                for i in done:
+                    add(i, 0, HALF, False)
+                quant_w(a)
+                weave_x(1, r - 2, 192)
+                quant_y(u, 0, c0, c0 + 256)
+                quant_w(a + 1)
+                quant_x(1, r - 2)
+            if r == 2:
+                load_w(12)
+                load_w(13)
+                load_f(1, 0, 0, 4)
+                load_x(1, 2)
+                load_w(14)
+                load_w(15)
+                load_x(1, 3)
+            if r == 3:
+                load_f(0, 1, 0, 4)
+                store_words(0, 0, 0, HALF)
+                store_y(1, 0, 0, 4, 0, HALF)
+                load_f(1, 1, 0, 4)
+            if r == 5:
+                store_words(1, 0, 0, HALF)
+                store_y(2, 0, 0, 4, 0, HALF)
+
+        mm_all(14, 0, HALF, 6)
+        mm_all(15, 0, HALF, 7)
+        mul(12, 0, HALF)
+        mul(13, 0, HALF)
+        add(12, 0, HALF, False)
+        add(13, 0, HALF, False)
+        weave_y(2, 0, True, 0, 320)
+        weave_y(2, 0, False, 320, HALF)
+        mul(14, 0, HALF)
+        mul(15, 0, HALF)
+        add(14, 0, HALF, False)
+        add(15, 0, HALF, False)
+        quant_y(2, 0, 0, HALF)
+        store_words(2, 0, 0, HALF)
+        store_y(3, 0, 0, 4, 0, HALF)
+
+        prev = (3, 0)
+        for u in range(3):
+            for i in range(4 * u, 4 * u + 4):
+                mm_all(i, HALF, HALF, i % 8)
+                mul(i, HALF, HALF)
+                if i % 4 == 0:
+                    weave_y(prev[0], prev[1], False, 352, HALF)
+                    weave_y(prev[0], prev[1], True, 0, 352)
+                add(i, HALF, HALF, False)
+                if i % 4 == 2:
+                    quant_y(prev[0], prev[1], 0, HALF)
+                    store_words(prev[0], prev[1], 0, HALF)
+                    if u == 2:
+                        store_scales(0, 0, PARTS * D, [nc.sync] * 4)
+                if i % 2 == 1:
+                    store_y(u, 1, i % 4 - 1, i % 4 + 1, 0, HALF)
+            prev = (u, 1)
+        for s in range(2):
+            c0 = 256 * s
+            for i in range(12, 16):
+                mm_all(i, HALF + c0, 256, (4 * s + i) % 8)
+                mul(i, HALF + c0, 256)
+                if i == 12 and s == 0:
+                    weave_y(2, 1, False, 352, HALF)
+                    weave_y(2, 1, True, 0, 352)
+                if i == 12 and s == 1:
+                    weave_y(3, 1, False, 176, 256)
+                    weave_y(3, 1, True, 0, 176)
+                add(i, HALF + c0, 256, False)
+                if i == 15 and s == 0:
+                    quant_y(2, 1, 0, HALF)
+                    store_words(2, 1, 0, HALF)
+                if i == 14 and s == 1:
+                    quant_y(3, 1, 0, 256)
+                    store_words(3, 1, 0, 256)
+                    store_scales(1, 0, PARTS * D - 256, [nc.sync] * 4)
+                if i % 2 == 1:
+                    store_y(3, 1, i % 4 - 1, i % 4 + 1, c0, c0 + 256)
+        weave_y(3, 1, False, 256 + 176, HALF)
+        weave_y(3, 1, True, 256, 256 + 176)
+        quant_y(3, 1, 256, HALF)
+        store_words(3, 1, 256, HALF)
+        store_scales(1, PARTS * D - 256, PARTS * D, [nc.scalar, nc.scalar, nc.sync, nc.sync])

@@ -20,6 +20,9 @@ K_PASS = P * PACK
 PASSES = T // K_PASS
 HALF = 512
 TILES = 16
+HS, X0S, XS, YS2, YS = 160, 320, 192, 256, 320
+LV, LS = 2, 352
+PIECES = [(0, 0, 512), (1, 0, 512), (2, 0, 256), (2, 256, 256), (3, 0, 256), (3, 256, 256)]
 W_RING, X_RING, WG_RING, XG_RING, Y_RING, YG_RING = 8, 4, 3, 3, 4, 3
 
 
@@ -87,10 +90,10 @@ def tile_nonuniform_fourier_filter_g2_kernel(tc, tokens, waves, filt, offset, ou
             else:
                 nc.scalar.copy(out=o, in_=s)
 
-        def weave_x(h, g, split):
-            x_grouped[h, g] = sb.tile([P, HALF, PACK], BF16, name="x_grouped%d" % ((4 * h + g) % XG_RING), align_bytes=64)
-            weave(False, x_grouped[h, g], x_raw[h, g], 0, split)
-            weave(True, x_grouped[h, g], x_raw[h, g], split, HALF)
+        def weave_x(h, g, on_vector, c0, c1):
+            if (h, g) not in x_grouped:
+                x_grouped[h, g] = sb.tile([P, HALF, PACK], BF16, name="x_grouped%d" % ((4 * h + g) % XG_RING), align_bytes=64)
+            weave(on_vector, x_grouped[h, g], x_raw[h, g], c0, c1)
 
         def quant_x(h, g):
             nc.vector.quantize_mx(out=x_codes[:, 4 * h + g, :].bitcast(FP8X4), scales=x_scales[:, 4 * h + g, :],
@@ -159,38 +162,45 @@ def tile_nonuniform_fourier_filter_g2_kernel(tc, tokens, waves, filt, offset, ou
 
         make_identity(nc, ident[:])
         nc.scalar.dma_start(out=off_raw[:], in_=offset.rearrange("c f -> (c f)").rearrange("(q p t) -> p q t", p=P, t=PACK))
+        load_w(0)
         for g in range(PASSES):
-            load_w(g)
+            load_w(g + 1)
             load_x(0, g)
-        load_w(4)
         load_w(5)
+        load_x(1, 0)
         load_w(6)
         load_f(0, 0, 0, 2)
         load_w(7)
         load_f(0, 0, 2, 4)
+        load_w(8)
+        load_w(9)
+        load_x(1, 1)
+        load_w(10)
+        load_w(11)
+        load_x(1, 2)
         nc.scalar.activation(out=off[:], in_=off_raw[:], func=IDENTITY)
 
         transpose_w(0)
+        transpose_w(1)
+        evac_w(0)
+        quant_w(0)
         for g in range(PASSES):
-            evac_w(g)
-            weave_x(0, g, 160)
-            quant_w(g)
+            evac_w(g + 1)
+            weave_x(0, g, False, 0, HS)
+            weave_x(0, g, True, HS, HALF)
+            quant_w(g + 1)
             quant_x(0, g)
-            transpose_w(g + 1)
-            if g == PASSES - 1:
-                transpose_w(5)
-            for gg in range(g):
-                mm(g, 0, HALF, gg, 4 + g)
-            for i in range(g + 1):
+            transpose_w(g + 2)
+            if 1 <= g <= 2:
+                for gg in range(g):
+                    mm(g + 1, 0, HALF, gg, 5 + g)
+            for i in range(min(g + 2, 4)):
                 mm(i, 0, HALF, g, 4 + i)
-        evac_w(4)
         evac_w(5)
-        quant_w(4)
+        weave_x(1, 0, False, 0, X0S)
+        weave_x(1, 0, True, X0S, HALF)
         quant_w(5)
 
-        load_w(8)
-        load_w(9)
-        load_x(1, 0)
         for r in range(1, 6):
             a, m = 2 * r + 4, 2 * r + 2
             done = [0, 1, 2, 3] if r == 1 else [2 * r, 2 * r + 1]
@@ -203,99 +213,96 @@ def tile_nonuniform_fourier_filter_g2_kernel(tc, tokens, waves, filt, offset, ou
             evac_w(a)
             evac_w(a + 1)
             if r == 1:
-                add(0, 0, HALF, True)
-                add(1, 0, HALF, True)
+                quant_x(1, 0)
                 quant_w(a)
+                add(0, 0, HALF, True)
+                add(1, 0, HALF, False)
                 add(2, 0, HALF, False)
                 add(3, 0, HALF, False)
                 quant_w(a + 1)
-                load_w(10)
-                load_w(11)
-                load_x(1, 1)
                 store_y(0, 0, 0, 4, 0, HALF)
-            else:
-                u, c0 = (r - 2) // 2, 256 * (r % 2)
-                weave_y(u, 0, True, c0, c0 + 256)
-                for i in done:
-                    add(i, 0, HALF, False)
-                quant_w(a)
-                weave_x(1, r - 2, 192)
-                quant_y(u, 0, c0, c0 + 256)
-                quant_w(a + 1)
-                quant_x(1, r - 2)
-            if r == 2:
+                load_f(1, 0, 0, 4)
                 load_w(12)
                 load_w(13)
-                load_f(1, 0, 0, 4)
-                load_x(1, 2)
+                load_x(1, 3)
                 load_w(14)
                 load_w(15)
-                load_x(1, 3)
-            if r == 3:
                 load_f(0, 1, 0, 4)
-                store_words(0, 0, 0, HALF)
+            else:
+                u, c0 = (r - 2) // 2, 256 * (r % 2)
+                for i in done:
+                    add(i, 0, HALF, False)
+                if r < 5:
+                    weave_x(1, r - 1, False, 0, XS)
+                    weave_x(1, r - 1, True, XS, HALF)
+                quant_w(a)
+                weave_y(u, 0, True, c0, c0 + 256)
+                quant_w(a + 1)
+                if r > 2:
+                    quant_x(1, r - 2)
+                quant_y(u, 0, c0, c0 + 256)
+            if r == 3:
                 store_y(1, 0, 0, 4, 0, HALF)
+                store_words(0, 0, 0, HALF)
                 load_f(1, 1, 0, 4)
             if r == 5:
-                store_words(1, 0, 0, HALF)
                 store_y(2, 0, 0, 4, 0, HALF)
+                store_words(1, 0, 0, HALF)
 
+        weave_y(2, 0, False, YS2, HALF)
         mm_all(14, 0, HALF, 6)
         mm_all(15, 0, HALF, 7)
         mul(12, 0, HALF)
         mul(13, 0, HALF)
         add(12, 0, HALF, False)
         add(13, 0, HALF, False)
-        weave_y(2, 0, True, 0, 320)
-        weave_y(2, 0, False, 320, HALF)
+        weave_y(2, 0, True, 0, YS2)
         mul(14, 0, HALF)
-        mul(15, 0, HALF)
         add(14, 0, HALF, False)
-        add(15, 0, HALF, False)
         quant_y(2, 0, 0, HALF)
+        mul(15, 0, HALF)
+        add(15, 0, HALF, False)
         store_words(2, 0, 0, HALF)
         store_y(3, 0, 0, 4, 0, HALF)
 
-        prev = (3, 0)
-        for u in range(3):
+        pieces = PIECES
+        prev = (3, 0, 0, HALF)
+        n = 0
+        for k, (u, c0, width) in enumerate(pieces):
+            pu, ph, p0, pw = prev
+            last = k == len(pieces) - 1
+            cut = p0 + (pw * YS // HALF) // 16 * 16
             for i in range(4 * u, 4 * u + 4):
-                mm_all(i, HALF, HALF, i % 8)
-                mul(i, HALF, HALF)
+                mm_all(i, HALF + c0, width, n % 8)
+                n += 1
+                mul(i, HALF + c0, width)
                 if i % 4 == 0:
-                    weave_y(prev[0], prev[1], False, 352, HALF)
-                    weave_y(prev[0], prev[1], True, 0, 352)
-                add(i, HALF, HALF, False)
-                if i % 4 == 2:
-                    quant_y(prev[0], prev[1], 0, HALF)
-                    store_words(prev[0], prev[1], 0, HALF)
-                    if u == 2:
+                    weave_y(pu, ph, False, cut, p0 + pw)
+                if i % 4 == 1:
+                    weave_y(pu, ph, True, p0, cut)
+                if not (last and i % 4 >= LV):
+                    add(i, HALF + c0, width, False)
+                if i % 4 == 3:
+                    if last:
+                        for ii in range(4 * u + LV, 4 * u + 4):
+                            add(ii, HALF + c0, width, True)
+                    quant_y(pu, ph, p0, p0 + pw)
+                    if pu == 3 and ph == 1:
+                        store_words(pu, ph, p0, p0 + pw)
+                    elif p0 + pw == HALF:
+                        store_words(pu, ph, 0, HALF)
+                    if (pu, ph) == (1, 1) and p0 + pw == HALF:
                         store_scales(0, 0, PARTS * D, [nc.sync] * 4)
-                if i % 2 == 1:
-                    store_y(u, 1, i % 4 - 1, i % 4 + 1, 0, HALF)
-            prev = (u, 1)
-        for s in range(2):
-            c0 = 256 * s
-            for i in range(12, 16):
-                mm_all(i, HALF + c0, 256, (4 * s + i) % 8)
-                mul(i, HALF + c0, 256)
-                if i == 12 and s == 0:
-                    weave_y(2, 1, False, 352, HALF)
-                    weave_y(2, 1, True, 0, 352)
-                if i == 12 and s == 1:
-                    weave_y(3, 1, False, 176, 256)
-                    weave_y(3, 1, True, 0, 176)
-                add(i, HALF + c0, 256, False)
-                if i == 15 and s == 0:
-                    quant_y(2, 1, 0, HALF)
-                    store_words(2, 1, 0, HALF)
-                if i == 14 and s == 1:
-                    quant_y(3, 1, 0, 256)
-                    store_words(3, 1, 0, 256)
-                    store_scales(1, 0, PARTS * D - 256, [nc.sync] * 4)
-                if i % 2 == 1:
-                    store_y(3, 1, i % 4 - 1, i % 4 + 1, c0, c0 + 256)
-        weave_y(3, 1, False, 256 + 176, HALF)
-        weave_y(3, 1, True, 256, 256 + 176)
-        quant_y(3, 1, 256, HALF)
-        store_words(3, 1, 256, HALF)
-        store_scales(1, PARTS * D - 256, PARTS * D, [nc.scalar, nc.scalar, nc.sync, nc.sync])
+                if (width == HALF or last) and i % 2 == 1:
+                    store_y(u, 1, i % 4 - 1, i % 4 + 1, c0, c0 + width)
+            if width < HALF and not last:
+                store_y(u, 1, 0, 4, c0, c0 + width)
+            prev = (u, 1, c0, width)
+        pu, ph, p0, pw = prev
+        cut = p0 + (pw * LS // HALF) // 16 * 16
+        if cut < HALF:
+            weave_y(pu, ph, False, cut, HALF)
+        weave_y(pu, ph, True, p0, cut)
+        quant_y(pu, ph, p0, HALF)
+        store_words(3, 1, p0, HALF)
+        store_scales(1, 0, PARTS * D, [nc.scalar, nc.scalar, nc.sync, nc.sync])

@@ -20,10 +20,10 @@ K_PASS = P * PACK
 PASSES = T // K_PASS
 HALF = 512
 TILES = 16
-HS, X0S, XS, YS2, YS = 160, 320, 192, 256, 320
-LV, LS = 2, 352
-PIECES = [(0, 0, 512), (1, 0, 512), (2, 0, 256), (2, 256, 256), (3, 0, 256), (3, 256, 256)]
-W_RING, X_RING, WG_RING, XG_RING, Y_RING, YG_RING = 8, 4, 3, 3, 4, 3
+HS, X0S, XS, YS2, YS = 160, 320, 192, 320, 352
+LV, LS = 2, 384
+PIECES = [(0,0,512),(1,0,512),(2,0,256),(2,256,256),(3,0,256),(3,256,256)]
+W_RING, X_RING, WG_RING, XG_RING, Y_RING, YG_RING = 4, 4, 3, 3, 4, 3
 
 
 def tile_nonuniform_fourier_filter_g2_kernel(tc, tokens, waves, filt, offset, out_0, out_1, out_2):
@@ -40,7 +40,7 @@ def tile_nonuniform_fourier_filter_g2_kernel(tc, tokens, waves, filt, offset, ou
         w_scales = sb.tile([P, TILES, PASSES * P], U8, name="w_scales", align_bytes=64)
         x_codes = sb.tile([P, 2 * PASSES, HALF], I32, name="x_codes", align_bytes=64)
         x_scales = sb.tile([P, 2 * PASSES, HALF], U8, name="x_scales", align_bytes=64)
-        filt_sb = sb.tile([P, 4, PACK, HALF], BF16, name="filt_sb", align_bytes=64)
+        filt_sb = sb.tile([P, 2, PACK, D], BF16, name="filt_sb", align_bytes=64)
         y_words = sb.tile([P, 2, PARTS * D], I32, name="y_words", align_bytes=64)
         y_scales = sb.tile([P, 2, PARTS * D], U8, name="y_scales", align_bytes=64)
 
@@ -49,23 +49,25 @@ def tile_nonuniform_fourier_filter_g2_kernel(tc, tokens, waves, filt, offset, ou
         def part_group(i):
             return (i // 4) % 2, i // 8, i % 4
 
-        def load_w(i):
+        def load_w(i, n=1):
             c, g, t = part_group(i)
-            w_raw[i] = sb.tile([P, T], BF16, name="w_raw%d" % (i % W_RING), align_bytes=64)
+            j = i // 2
+            if j not in w_raw:
+                w_raw[j] = sb.tile([P, 2, T], BF16, name="w_raw%d" % (j % W_RING), align_bytes=64)
             rows = waves[c, g * K_PASS:(g + 1) * K_PASS, :].rearrange("(m t) k -> m t k", t=PACK)
-            nc.sync.dma_start(out=w_raw[i][:], in_=rows[:, t, :])
+            nc.sync.dma_start(out=w_raw[j][:, i % 2:i % 2 + n, :], in_=rows[:, t:t + n, :])
 
         def load_x(h, g):
             x_raw[h, g] = sb.tile([P, PACK, HALF], BF16, name="x_raw%d" % (g % X_RING), align_bytes=64)
             rows = tokens[g * K_PASS:(g + 1) * K_PASS, h * HALF:(h + 1) * HALF]
             nc.sync.dma_start(out=x_raw[h, g][:], in_=rows.rearrange("(p j) w -> p j w", j=PACK))
 
-        def load_f(g, h, t0, t1):
-            rows = filt[g * K_PASS:(g + 1) * K_PASS, h * HALF:(h + 1) * HALF].rearrange("(p t) d -> p t d", t=PACK)
-            nc.sync.dma_start(out=filt_sb[:, 2 * g + h, t0:t1, :], in_=rows[:, t0:t1, :])
+        def load_f(g, d0, d1, t0, t1):
+            rows = filt[g * K_PASS:(g + 1) * K_PASS, d0:d1].rearrange("(p t) d -> p t d", t=PACK)
+            nc.sync.dma_start(out=filt_sb[:, g, t0:t1, d0:d1], in_=rows[:, t0:t1, :])
 
         def transpose_w(i):
-            words = w_raw[i][:].bitcast(F32)
+            words = w_raw[i // 2][:, i % 2, :].bitcast(F32)
             for b in range(2):
                 w_bank[i, b] = ps.tile([P, 2, 2, P], F32, name="bank%d" % (2 * (i % 2) + b))
                 for gg in range(2):
@@ -83,8 +85,8 @@ def tile_nonuniform_fourier_filter_g2_kernel(tc, tokens, waves, filt, offset, ou
                                   in_=w_grouped[i][:].rearrange("p g r u -> p (g r u)").bitcast(BF16))
 
         def weave(on_vector, dst, src, c0, c1):
-            o = dst[:, c0:c1, :].rearrange("p (c i) t -> p c t i", i=4)
-            s = src[:, :, c0:c1].rearrange("p t (c i) -> p c t i", i=4)
+            o = dst[:, c0:c1, :]
+            s = src[:, :, c0:c1].rearrange("p t c -> p c t")
             if on_vector:
                 nc.vector.tensor_copy(out=o, in_=s)
             else:
@@ -121,7 +123,7 @@ def tile_nonuniform_fourier_filter_g2_kernel(tc, tokens, waves, filt, offset, ou
             if unit not in y:
                 y[unit] = sb.tile([P, PACK, HALF], F32, name="y%d" % (len(y) % Y_RING), align_bytes=64)
             nc.vector.tensor_tensor(out=y[unit][:, t, c0:c0 + width], in0=acc[i, d0][:],
-                                    in1=filt_sb[:, 2 * g + h, t, c0:c0 + width], op=ALU.mult)
+                                    in1=filt_sb[:, g, t, d0:d0 + width], op=ALU.mult)
 
         def add(i, d0, width, on_vector):
             c, g, t = part_group(i)
@@ -169,14 +171,12 @@ def tile_nonuniform_fourier_filter_g2_kernel(tc, tokens, waves, filt, offset, ou
         load_w(5)
         load_x(1, 0)
         load_w(6)
-        load_f(0, 0, 0, 2)
         load_w(7)
-        load_f(0, 0, 2, 4)
-        load_w(8)
-        load_w(9)
+        load_f(0, 0, HALF, 0, 2)
+        load_f(0, 0, HALF, 2, 4)
+        load_w(8, 2)
         load_x(1, 1)
-        load_w(10)
-        load_w(11)
+        load_w(10, 2)
         load_x(1, 2)
         nc.scalar.activation(out=off[:], in_=off_raw[:], func=IDENTITY)
 
@@ -220,14 +220,13 @@ def tile_nonuniform_fourier_filter_g2_kernel(tc, tokens, waves, filt, offset, ou
                 add(2, 0, HALF, False)
                 add(3, 0, HALF, False)
                 quant_w(a + 1)
-                store_y(0, 0, 0, 4, 0, HALF)
-                load_f(1, 0, 0, 4)
-                load_w(12)
-                load_w(13)
+                load_f(1, 0, D, 0, 2)
+                load_w(12, 2)
                 load_x(1, 3)
-                load_w(14)
-                load_w(15)
-                load_f(0, 1, 0, 4)
+                load_f(1, 0, D, 2, 4)
+                load_w(14, 2)
+                store_y(0, 0, 0, 4, 0, HALF)
+                load_f(0, HALF, D, 0, 4)
             else:
                 u, c0 = (r - 2) // 2, 256 * (r % 2)
                 for i in done:
@@ -244,7 +243,6 @@ def tile_nonuniform_fourier_filter_g2_kernel(tc, tokens, waves, filt, offset, ou
             if r == 3:
                 store_y(1, 0, 0, 4, 0, HALF)
                 store_words(0, 0, 0, HALF)
-                load_f(1, 1, 0, 4)
             if r == 5:
                 store_y(2, 0, 0, 4, 0, HALF)
                 store_words(1, 0, 0, HALF)
@@ -293,10 +291,8 @@ def tile_nonuniform_fourier_filter_g2_kernel(tc, tokens, waves, filt, offset, ou
                         store_words(pu, ph, 0, HALF)
                     if (pu, ph) == (1, 1) and p0 + pw == HALF:
                         store_scales(0, 0, PARTS * D, [nc.sync] * 4)
-                if (width == HALF or last) and i % 2 == 1:
+                if i % 2 == 1:
                     store_y(u, 1, i % 4 - 1, i % 4 + 1, c0, c0 + width)
-            if width < HALF and not last:
-                store_y(u, 1, 0, 4, c0, c0 + width)
             prev = (u, 1, c0, width)
         pu, ph, p0, pw = prev
         cut = p0 + (pw * LS // HALF) // 16 * 16

@@ -20,9 +20,14 @@ K_PASS = P * PACK
 PASSES = T // K_PASS
 HALF = 512
 TILES = 16
-HS, X0S, XS, YS2, YS = 160, 320, 192, 320, 352
-LV, LS = 2, 384
+HS = 160
+YS = 336
+LV = 2
+LS = 384
 PIECES = [(0,0,512),(1,0,512),(2,0,256),(2,256,256),(3,0,256),(3,256,256)]
+LOADS = [("x",0,0),("w",6,1),("w",7,1),("f",0,2),("f",2,4),("w",8,2),("x",1,0),("w",10,2),("w",12,2),("x",2,0),("g",0,2),("w",14,2),("x",3,0),("g",2,4)]
+JOBS = ["Xv0 Wv6 av0 as1 as2 as3 sv9 Wv7","as4 as5 xs1,0,256 xv1,256,512 Wv8 yv0,0,256 sv11 Wv9 Yv0,0,256","as6 as7 xs2,0,256 xv2,256,512 Wv10 sv13 yv0,256,512 Wv11 Xv1 Yv0,256,512 ov0","as8 as9 xs3,0,256 xv3,256,512 Wv12 sv15 yv1,0,256 Wv13 Xv2 Yv1,0,256 fv0 ov1 wv0","as10 as11 Wv14 yv1,256,512 Wv15 Xv3 Yv1,256,512 ov2 wv1","ys2,320,512 mv12 mv13 as12 as13 yv2,0,320","mv14 as14 Yv2,0,512 mv15 as15 wv2 ov3"]
+JOB0 = "xs0,0,320 xv0,320,512 Wv5 sv7"
 W_RING, X_RING, WG_RING, XG_RING, Y_RING, YG_RING = 4, 4, 3, 3, 4, 3
 
 
@@ -34,7 +39,7 @@ def tile_nonuniform_fourier_filter_g2_kernel(tc, tokens, waves, filt, offset, ou
         ctx.enter_context(tc.manual_schedule())
 
         ident = sb.tile([P, P], F32, name="ident", align_bytes=64)
-        off_raw = sb.tile([P, 4, PACK], BF16, name="off_raw")
+        off_rows = sb.tile([P, 256], F32, name="off_rows", align_bytes=64)
         off = sb.tile([P, 4, PACK], F32, name="off")
         w_codes = sb.tile([P, TILES, PASSES * P], I32, name="w_codes", align_bytes=64)
         w_scales = sb.tile([P, TILES, PASSES * P], U8, name="w_scales", align_bytes=64)
@@ -45,6 +50,8 @@ def tile_nonuniform_fourier_filter_g2_kernel(tc, tokens, waves, filt, offset, ou
         y_scales = sb.tile([P, 2, PARTS * D], U8, name="y_scales", align_bytes=64)
 
         w_raw, x_raw, w_bank, w_grouped, x_grouped, acc, y, y_grouped = {}, {}, {}, {}, {}, {}, {}, {}
+
+        w_sorted = {}
 
         def part_group(i):
             return (i // 4) % 2, i // 8, i % 4
@@ -66,6 +73,16 @@ def tile_nonuniform_fourier_filter_g2_kernel(tc, tokens, waves, filt, offset, ou
             rows = filt[g * K_PASS:(g + 1) * K_PASS, d0:d1].rearrange("(p t) d -> p t d", t=PACK)
             nc.sync.dma_start(out=filt_sb[:, g, t0:t1, d0:d1], in_=rows[:, t0:t1, :])
 
+        def sort_w(i, on_vector):
+            w_sorted[i] = sb.tile([P, PASSES, 2, P], F32, name="w_sorted%d" % (len(w_sorted) % 2), align_bytes=64)
+            if on_vector:
+                words = w_raw[i // 2][:, i % 2, :].bitcast(F32)
+                nc.vector.tensor_copy(out=w_sorted[i][:], in_=words.rearrange("m (g p u) -> m g u p", g=PASSES, u=2))
+            else:
+                for g in range(0, PASSES, 2):
+                    words = w_raw[i // 2][:, i % 2, g * K_PASS:(g + 2) * K_PASS].bitcast(F32)
+                    nc.scalar.copy(out=w_sorted[i][:, g:g + 2, :, :], in_=words.rearrange("m (g p u) -> m g u p", g=2, u=2))
+
         def transpose_w(i):
             words = w_raw[i // 2][:, i % 2, :].bitcast(F32)
             for b in range(2):
@@ -73,7 +90,8 @@ def tile_nonuniform_fourier_filter_g2_kernel(tc, tokens, waves, filt, offset, ou
                 for gg in range(2):
                     g = 2 * b + gg
                     for u in range(2):
-                        nc.tensor.transpose(w_bank[i, b][:, gg, u, :], words[:, 256 * g + u:256 * (g + 1):2], ident[:])
+                        src = w_sorted[i][:, g, u, :] if i in w_sorted else words[:, 256 * g + u:256 * (g + 1):2]
+                        nc.tensor.transpose(w_bank[i, b][:, gg, u, :], src, ident[:])
 
         def evac_w(i):
             w_grouped[i] = sb.tile([P, PASSES, P, 2], F32, name="w_grouped%d" % (i % WG_RING), align_bytes=64)
@@ -85,8 +103,8 @@ def tile_nonuniform_fourier_filter_g2_kernel(tc, tokens, waves, filt, offset, ou
                                   in_=w_grouped[i][:].rearrange("p g r u -> p (g r u)").bitcast(BF16))
 
         def weave(on_vector, dst, src, c0, c1):
-            o = dst[:, c0:c1, :]
-            s = src[:, :, c0:c1].rearrange("p t c -> p c t")
+            o = dst[:, c0:c1, :].rearrange("p (c i) t -> p c t i", i=4)
+            s = src[:, :, c0:c1].rearrange("p t (c i) -> p c t i", i=4)
             if on_vector:
                 nc.vector.tensor_copy(out=o, in_=s)
             else:
@@ -162,23 +180,28 @@ def tile_nonuniform_fourier_filter_g2_kernel(tc, tokens, waves, filt, offset, ou
                 queues[q].dma_start(out=out_2[g, 4 * q:4 * q + 4, m0:m1].bitcast(I32),
                                     in_=y_scales[32 * q:32 * q + 4, g, m0:m1].bitcast(I32))
 
+        nc.gpsimd.memset(off_rows[:], 0.0)
         make_identity(nc, ident[:])
-        nc.scalar.dma_start(out=off_raw[:], in_=offset.rearrange("c f -> (c f)").rearrange("(q p t) -> p q t", p=P, t=PACK))
         load_w(0)
+        nc.sync.dma_start(out=off_rows[0:4, :], in_=offset.rearrange("c (g k) -> (c g) k", g=2).bitcast(F32))
         for g in range(PASSES):
             load_w(g + 1)
             load_x(0, g)
         load_w(5)
-        load_x(1, 0)
-        load_w(6)
-        load_w(7)
-        load_f(0, 0, HALF, 0, 2)
-        load_f(0, 0, HALF, 2, 4)
-        load_w(8, 2)
-        load_x(1, 1)
-        load_w(10, 2)
-        load_x(1, 2)
-        nc.scalar.activation(out=off[:], in_=off_raw[:], func=IDENTITY)
+        for kind, a, b in LOADS:
+            if kind == "w":
+                load_w(a, b)
+            elif kind == "x":
+                load_x(1, a)
+            elif kind == "f":
+                load_f(0, 0, HALF, a, b)
+            else:
+                load_f(1, 0, D, a, b)
+        off_bank = ps.tile([P, 2, P], F32, name="bank7")
+        for u in range(2):
+            nc.tensor.transpose(off_bank[:, u, :], off_rows[:, u:256:2], ident[:])
+        nc.scalar.activation(out=off[:].rearrange("p q (u e) -> p q u e", u=2),
+                             in_=off_bank[:, :, 0:4].bitcast(BF16).rearrange("p u (q e) -> p q u e", e=2), func=IDENTITY)
 
         transpose_w(0)
         transpose_w(1)
@@ -197,10 +220,34 @@ def tile_nonuniform_fourier_filter_g2_kernel(tc, tokens, waves, filt, offset, ou
             for i in range(min(g + 2, 4)):
                 mm(i, 0, HALF, g, 4 + i)
         evac_w(5)
-        weave_x(1, 0, False, 0, X0S)
-        weave_x(1, 0, True, X0S, HALF)
-        quant_w(5)
 
+        def jobs(text):
+            for job in text.split():
+                k, on_vector, n = job[0], job[1] == "v", [int(z) for z in job[2:].split(",")]
+                if k == "s":
+                    sort_w(n[0], on_vector)
+                elif k == "x":
+                    weave_x(1, n[0], on_vector, n[1], n[2])
+                elif k == "X":
+                    quant_x(1, n[0])
+                elif k == "y":
+                    weave_y(n[0], 0, on_vector, n[1], n[2])
+                elif k == "Y":
+                    quant_y(n[0], 0, n[1], n[2])
+                elif k == "W":
+                    quant_w(n[0])
+                elif k == "a":
+                    add(n[0], 0, HALF, on_vector)
+                elif k == "m":
+                    mul(n[0], 0, HALF)
+                elif k == "o":
+                    store_y(n[0], 0, 0, 4, 0, HALF)
+                elif k == "w":
+                    store_words(n[0], 0, 0, HALF)
+                elif k == "f":
+                    load_f(0, HALF, D, 0, 4)
+
+        jobs(JOB0)
         for r in range(1, 6):
             a, m = 2 * r + 4, 2 * r + 2
             done = [0, 1, 2, 3] if r == 1 else [2 * r, 2 * r + 1]
@@ -212,57 +259,13 @@ def tile_nonuniform_fourier_filter_g2_kernel(tc, tokens, waves, filt, offset, ou
             mm_all(m + 1, 0, HALF, 4 + (m + 1) % 4)
             evac_w(a)
             evac_w(a + 1)
-            if r == 1:
-                quant_x(1, 0)
-                quant_w(a)
-                add(0, 0, HALF, True)
-                add(1, 0, HALF, False)
-                add(2, 0, HALF, False)
-                add(3, 0, HALF, False)
-                quant_w(a + 1)
-                load_f(1, 0, D, 0, 2)
-                load_w(12, 2)
-                load_x(1, 3)
-                load_f(1, 0, D, 2, 4)
-                load_w(14, 2)
-                store_y(0, 0, 0, 4, 0, HALF)
-                load_f(0, HALF, D, 0, 4)
-            else:
-                u, c0 = (r - 2) // 2, 256 * (r % 2)
-                for i in done:
-                    add(i, 0, HALF, False)
-                if r < 5:
-                    weave_x(1, r - 1, False, 0, XS)
-                    weave_x(1, r - 1, True, XS, HALF)
-                quant_w(a)
-                weave_y(u, 0, True, c0, c0 + 256)
-                quant_w(a + 1)
-                if r > 2:
-                    quant_x(1, r - 2)
-                quant_y(u, 0, c0, c0 + 256)
-            if r == 3:
-                store_y(1, 0, 0, 4, 0, HALF)
-                store_words(0, 0, 0, HALF)
-            if r == 5:
-                store_y(2, 0, 0, 4, 0, HALF)
-                store_words(1, 0, 0, HALF)
-
-        weave_y(2, 0, False, YS2, HALF)
+            jobs(JOBS[r - 1])
         mm_all(14, 0, HALF, 6)
         mm_all(15, 0, HALF, 7)
-        mul(12, 0, HALF)
-        mul(13, 0, HALF)
-        add(12, 0, HALF, False)
-        add(13, 0, HALF, False)
-        weave_y(2, 0, True, 0, YS2)
-        mul(14, 0, HALF)
-        add(14, 0, HALF, False)
-        quant_y(2, 0, 0, HALF)
-        mul(15, 0, HALF)
-        add(15, 0, HALF, False)
-        store_words(2, 0, 0, HALF)
-        store_y(3, 0, 0, 4, 0, HALF)
-
+        jobs(JOBS[5])
+        for i in range(4):
+            mm_all(i, HALF, HALF, i)
+        jobs(JOBS[6])
         pieces = PIECES
         prev = (3, 0, 0, HALF)
         n = 0
@@ -271,7 +274,8 @@ def tile_nonuniform_fourier_filter_g2_kernel(tc, tokens, waves, filt, offset, ou
             last = k == len(pieces) - 1
             cut = p0 + (pw * YS // HALF) // 16 * 16
             for i in range(4 * u, 4 * u + 4):
-                mm_all(i, HALF + c0, width, n % 8)
+                if k > 0:
+                    mm_all(i, HALF + c0, width, n % 8)
                 n += 1
                 mul(i, HALF + c0, width)
                 if i % 4 == 0:

from contextlib import ExitStack

import concourse.mybir as mybir
from concourse.masks import make_identity

PARTS, T, F, D = 2, 2048, 1024, 1024
FLOPS = 2 * PARTS * F * T * D

F32 = mybir.dt.float32
BF16 = mybir.dt.bfloat16
I32 = mybir.dt.int32
U8 = mybir.dt.uint8
FP8X4 = mybir.dt.float8_e4m3fn_x4
ALU = mybir.AluOpType
IDENTITY = mybir.ActivationFunctionType.Identity

P = 128
PACK = 4
K_PASS = P * PACK
PASSES = T // K_PASS
HALF = 512
TILES = 16
HS = 160
YS = 336
LV = 2
LS = 384
PIECES = [(0,0,512),(1,0,512),(2,0,256),(2,256,256),(3,0,256),(3,256,256)]
LOADS = [("x",0,0),("w",6,1),("w",7,1),("f",0,2),("f",2,4),("w",8,2),("x",1,0),("w",10,2),("w",12,2),("x",2,0),("g",0,2),("w",14,2),("x",3,0),("g",2,4)]
JOBS = ["Xv0 Wv6 av0 as1 as2 as3 sv9 Wv7","as4 as5 xs1,0,256 xv1,256,512 Wv8 yv0,0,256 sv11 Wv9 Yv0,0,256","as6 as7 xs2,0,256 xv2,256,512 Wv10 sv13 yv0,256,512 Wv11 Xv1 Yv0,256,512 ov0","as8 as9 xs3,0,256 xv3,256,512 Wv12 sv15 yv1,0,256 Wv13 Xv2 Yv1,0,256 fv0 ov1 wv0","as10 as11 Wv14 yv1,256,512 Wv15 Xv3 Yv1,256,512 ov2 wv1","ys2,320,512 mv12 mv13 as12 as13 yv2,0,320","mv14 as14 Yv2,0,512 mv15 as15 wv2 ov3"]
JOB0 = "xs0,0,320 xv0,320,512 Wv5 sv7"
W_RING, X_RING, WG_RING, XG_RING, Y_RING, YG_RING = 4, 4, 3, 3, 4, 3


def tile_nonuniform_fourier_filter_g2_kernel(tc, tokens, waves, filt, offset, out_0, out_1, out_2):
    nc = tc.nc
    with ExitStack() as ctx:
        sb = ctx.enter_context(tc.tile_pool(name="sb", bufs=1))
        ps = ctx.enter_context(tc.psum_pool(name="ps", bufs=1))
        ctx.enter_context(tc.manual_schedule())

        ident = sb.tile([P, P], F32, name="ident", align_bytes=64)
        off_rows = sb.tile([P, 256], F32, name="off_rows", align_bytes=64)
        off = sb.tile([P, 4, PACK], F32, name="off")
        w_codes = sb.tile([P, TILES, PASSES * P], I32, name="w_codes", align_bytes=64)
        w_scales = sb.tile([P, TILES, PASSES * P], U8, name="w_scales", align_bytes=64)
        x_codes = sb.tile([P, 2 * PASSES, HALF], I32, name="x_codes", align_bytes=64)
        x_scales = sb.tile([P, 2 * PASSES, HALF], U8, name="x_scales", align_bytes=64)
        filt_sb = sb.tile([P, 2, PACK, D], BF16, name="filt_sb", align_bytes=64)
        y_words = sb.tile([P, 2, PARTS * D], I32, name="y_words", align_bytes=64)
        y_scales = sb.tile([P, 2, PARTS * D], U8, name="y_scales", align_bytes=64)

        w_raw, x_raw, w_bank, w_grouped, x_grouped, acc, y, y_grouped = {}, {}, {}, {}, {}, {}, {}, {}

        w_sorted = {}

        def part_group(i):
            return (i // 4) % 2, i // 8, i % 4

        def load_w(i, n=1):
            c, g, t = part_group(i)
            j = i // 2
            if j not in w_raw:
                w_raw[j] = sb.tile([P, 2, T], BF16, name="w_raw%d" % (j % W_RING), align_bytes=64)
            rows = waves[c, g * K_PASS:(g + 1) * K_PASS, :].rearrange("(m t) k -> m t k", t=PACK)
            nc.sync.dma_start(out=w_raw[j][:, i % 2:i % 2 + n, :], in_=rows[:, t:t + n, :])

        def load_x(h, g):
            x_raw[h, g] = sb.tile([P, PACK, HALF], BF16, name="x_raw%d" % (g % X_RING), align_bytes=64)
            rows = tokens[g * K_PASS:(g + 1) * K_PASS, h * HALF:(h + 1) * HALF]
            nc.sync.dma_start(out=x_raw[h, g][:], in_=rows.rearrange("(p j) w -> p j w", j=PACK))

        def load_f(g, d0, d1, t0, t1):
            rows = filt[g * K_PASS:(g + 1) * K_PASS, d0:d1].rearrange("(p t) d -> p t d", t=PACK)
            nc.sync.dma_start(out=filt_sb[:, g, t0:t1, d0:d1], in_=rows[:, t0:t1, :])

        def sort_w(i, on_vector):
            w_sorted[i] = sb.tile([P, PASSES, 2, P], F32, name="w_sorted%d" % (len(w_sorted) % 2), align_bytes=64)
            if on_vector:
                words = w_raw[i // 2][:, i % 2, :].bitcast(F32)
                nc.vector.tensor_copy(out=w_sorted[i][:], in_=words.rearrange("m (g p u) -> m g u p", g=PASSES, u=2))
            else:
                for g in range(0, PASSES, 2):
                    words = w_raw[i // 2][:, i % 2, g * K_PASS:(g + 2) * K_PASS].bitcast(F32)
                    nc.scalar.copy(out=w_sorted[i][:, g:g + 2, :, :], in_=words.rearrange("m (g p u) -> m g u p", g=2, u=2))

        def transpose_w(i):
            words = w_raw[i // 2][:, i % 2, :].bitcast(F32)
            for b in range(2):
                w_bank[i, b] = ps.tile([P, 2, 2, P], F32, name="bank%d" % (2 * (i % 2) + b))
                for gg in range(2):
                    g = 2 * b + gg
                    for u in range(2):
                        src = w_sorted[i][:, g, u, :] if i in w_sorted else words[:, 256 * g + u:256 * (g + 1):2]
                        nc.tensor.transpose(w_bank[i, b][:, gg, u, :], src, ident[:])

        def evac_w(i):
            w_grouped[i] = sb.tile([P, PASSES, P, 2], F32, name="w_grouped%d" % (i % WG_RING), align_bytes=64)
            for b in range(2):
                nc.scalar.copy(out=w_grouped[i][:, 2 * b:2 * b + 2, :, :], in_=w_bank[i, b][:].rearrange("p g u r -> p g r u"))

        def quant_w(i):
            nc.vector.quantize_mx(out=w_codes[:, i, :].bitcast(FP8X4), scales=w_scales[:, i, :],
                                  in_=w_grouped[i][:].rearrange("p g r u -> p (g r u)").bitcast(BF16))

        def weave(on_vector, dst, src, c0, c1):
            o = dst[:, c0:c1, :].rearrange("p (c i) t -> p c t i", i=4)
            s = src[:, :, c0:c1].rearrange("p t (c i) -> p c t i", i=4)
            if on_vector:
                nc.vector.tensor_copy(out=o, in_=s)
            else:
                nc.scalar.copy(out=o, in_=s)

        def weave_x(h, g, on_vector, c0, c1):
            if (h, g) not in x_grouped:
                x_grouped[h, g] = sb.tile([P, HALF, PACK], BF16, name="x_grouped%d" % ((4 * h + g) % XG_RING), align_bytes=64)
            weave(on_vector, x_grouped[h, g], x_raw[h, g], c0, c1)

        def quant_x(h, g):
            nc.vector.quantize_mx(out=x_codes[:, 4 * h + g, :].bitcast(FP8X4), scales=x_scales[:, 4 * h + g, :],
                                  in_=x_grouped[h, g][:].rearrange("p w j -> p (w j)"))

        def mm(i, d0, width, g, bank):
            h, c0 = divmod(d0, HALF)
            if g == 0:
                acc[i, d0] = ps.tile([P, width], F32, name="bank%d" % bank)
            nc.tensor.matmul_mx(out=acc[i, d0][:],
                                lhsT=w_codes[:, i, g * P:(g + 1) * P].bitcast(FP8X4),
                                lhsT_scale=w_scales[:, i, g * P:(g + 1) * P],
                                rhs=x_codes[:, 4 * h + g, c0:c0 + width].bitcast(FP8X4),
                                rhs_scale=x_scales[:, 4 * h + g, c0:c0 + width],
                                start=(g == 0), stop=(g == PASSES - 1))

        def mm_all(i, d0, width, bank):
            for g in range(PASSES):
                mm(i, d0, width, g, bank)

        def mul(i, d0, width):
            c, g, t = part_group(i)
            h, c0 = divmod(d0, HALF)
            unit = (i // 4, h)
            if unit not in y:
                y[unit] = sb.tile([P, PACK, HALF], F32, name="y%d" % (len(y) % Y_RING), align_bytes=64)
            nc.vector.tensor_tensor(out=y[unit][:, t, c0:c0 + width], in0=acc[i, d0][:],
                                    in1=filt_sb[:, g, t, d0:d0 + width], op=ALU.mult)

        def add(i, d0, width, on_vector):
            c, g, t = part_group(i)
            h, c0 = divmod(d0, HALF)
            v = y[i // 4, h][:, t, c0:c0 + width]
            col = off[:, 2 * c + g, t:t + 1]
            if on_vector:
                nc.vector.tensor_scalar(out=v, in0=v, scalar1=col, scalar2=None, op0=ALU.add)
            else:
                nc.scalar.activation(out=v, in_=v, func=IDENTITY, bias=col, scale=1.0)

        def store_y(u, h, t0, t1, c0, c1):
            c, g, t = part_group(4 * u)
            rows = out_0[c, g * K_PASS:(g + 1) * K_PASS, h * HALF + c0:h * HALF + c1].rearrange("(p t) d -> p t d", t=PACK)
            nc.sync.dma_start(out=rows[:, t0:t1, :], in_=y[u, h][:, t0:t1, c0:c1])

        def weave_y(u, h, on_vector, c0, c1):
            if (u, h) not in y_grouped:
                y_grouped[u, h] = sb.tile([P, HALF, PACK], BF16, name="y_grouped%d" % (len(y_grouped) % YG_RING), align_bytes=64)
            weave(on_vector, y_grouped[u, h], y[u, h], c0, c1)

        def quant_y(u, h, c0, c1):
            c, g, t = part_group(4 * u)
            m0 = c * D + h * HALF
            nc.vector.quantize_mx(out=y_words[:, g, m0 + c0:m0 + c1].bitcast(FP8X4), scales=y_scales[:, g, m0 + c0:m0 + c1],
                                  in_=y_grouped[u, h][:, c0:c1, :].rearrange("p w j -> p (w j)"))

        def store_words(u, h, c0, c1):
            c, g, t = part_group(4 * u)
            m0 = c * D + h * HALF
            dst = out_1[g].rearrange("p m t -> p (m t)").bitcast(I32)
            nc.sync.dma_start(out=dst[:, m0 + c0:m0 + c1], in_=y_words[:, g, m0 + c0:m0 + c1])

        def store_scales(g, m0, m1, queues):
            for q in range(4):
                queues[q].dma_start(out=out_2[g, 4 * q:4 * q + 4, m0:m1].bitcast(I32),
                                    in_=y_scales[32 * q:32 * q + 4, g, m0:m1].bitcast(I32))

        nc.gpsimd.memset(off_rows[:], 0.0)
        make_identity(nc, ident[:])
        load_w(0)
        nc.sync.dma_start(out=off_rows[0:4, :], in_=offset.rearrange("c (g k) -> (c g) k", g=2).bitcast(F32))
        for g in range(PASSES):
            load_w(g + 1)
            load_x(0, g)
        load_w(5)
        for kind, a, b in LOADS:
            if kind == "w":
                load_w(a, b)
            elif kind == "x":
                load_x(1, a)
            elif kind == "f":
                load_f(0, 0, HALF, a, b)
            else:
                load_f(1, 0, D, a, b)
        off_bank = ps.tile([P, 2, P], F32, name="bank7")
        for u in range(2):
            nc.tensor.transpose(off_bank[:, u, :], off_rows[:, u:256:2], ident[:])
        nc.scalar.activation(out=off[:].rearrange("p q (u e) -> p q u e", u=2),
                             in_=off_bank[:, :, 0:4].bitcast(BF16).rearrange("p u (q e) -> p q u e", e=2), func=IDENTITY)

        transpose_w(0)
        transpose_w(1)
        evac_w(0)
        quant_w(0)
        for g in range(PASSES):
            evac_w(g + 1)
            weave_x(0, g, False, 0, HS)
            weave_x(0, g, True, HS, HALF)
            quant_w(g + 1)
            quant_x(0, g)
            transpose_w(g + 2)
            if 1 <= g <= 2:
                for gg in range(g):
                    mm(g + 1, 0, HALF, gg, 5 + g)
            for i in range(min(g + 2, 4)):
                mm(i, 0, HALF, g, 4 + i)
        evac_w(5)

        def jobs(text):
            for job in text.split():
                k, on_vector, n = job[0], job[1] == "v", [int(z) for z in job[2:].split(",")]
                if k == "s":
                    sort_w(n[0], on_vector)
                elif k == "x":
                    weave_x(1, n[0], on_vector, n[1], n[2])
                elif k == "X":
                    quant_x(1, n[0])
                elif k == "y":
                    weave_y(n[0], 0, on_vector, n[1], n[2])
                elif k == "Y":
                    quant_y(n[0], 0, n[1], n[2])
                elif k == "W":
                    quant_w(n[0])
                elif k == "a":
                    add(n[0], 0, HALF, on_vector)
                elif k == "m":
                    mul(n[0], 0, HALF)
                elif k == "o":
                    store_y(n[0], 0, 0, 4, 0, HALF)
                elif k == "w":
                    store_words(n[0], 0, 0, HALF)
                elif k == "f":
                    load_f(0, HALF, D, 0, 4)

        jobs(JOB0)
        for r in range(1, 6):
            a, m = 2 * r + 4, 2 * r + 2
            done = [0, 1, 2, 3] if r == 1 else [2 * r, 2 * r + 1]
            transpose_w(a)
            transpose_w(a + 1)
            for i in done:
                mul(i, 0, HALF)
            mm_all(m, 0, HALF, 4 + m % 4)
            mm_all(m + 1, 0, HALF, 4 + (m + 1) % 4)
            evac_w(a)
            evac_w(a + 1)
            jobs(JOBS[r - 1])
        mm_all(14, 0, HALF, 6)
        mm_all(15, 0, HALF, 7)
        jobs(JOBS[5])
        for i in range(4):
            mm_all(i, HALF, HALF, i)
        jobs(JOBS[6])
        pieces = PIECES
        prev = (3, 0, 0, HALF)
        n = 0
        for k, (u, c0, width) in enumerate(pieces):
            pu, ph, p0, pw = prev
            last = k == len(pieces) - 1
            cut = p0 + (pw * YS // HALF) // 16 * 16
            for i in range(4 * u, 4 * u + 4):
                if k > 0:
                    mm_all(i, HALF + c0, width, n % 8)
                n += 1
                mul(i, HALF + c0, width)
                if i % 4 == 0:
                    weave_y(pu, ph, False, cut, p0 + pw)
                if i % 4 == 1:
                    weave_y(pu, ph, True, p0, cut)
                if not (last and i % 4 >= LV):
                    add(i, HALF + c0, width, False)
                if i % 4 == 3:
                    if last:
                        for ii in range(4 * u + LV, 4 * u + 4):
                            add(ii, HALF + c0, width, True)
                    quant_y(pu, ph, p0, p0 + pw)
                    if pu == 3 and ph == 1:
                        store_words(pu, ph, p0, p0 + pw)
                    elif p0 + pw == HALF:
                        store_words(pu, ph, 0, HALF)
                    if (pu, ph) == (1, 1) and p0 + pw == HALF:
                        store_scales(0, 0, PARTS * D, [nc.sync] * 4)
                if i % 2 == 1:
                    store_y(u, 1, i % 4 - 1, i % 4 + 1, c0, c0 + width)
            prev = (u, 1, c0, width)
        pu, ph, p0, pw = prev
        cut = p0 + (pw * LS // HALF) // 16 * 16
        if cut < HALF:
            weave_y(pu, ph, False, cut, HALF)
        weave_y(pu, ph, True, p0, cut)
        quant_y(pu, ph, p0, HALF)
        store_words(3, 1, p0, HALF)
        store_scales(1, 0, PARTS * D, [nc.scalar, nc.scalar, nc.sync, nc.sync])
